import numpy as np, ml_dtypes
CORES = [9,13,81,85,89,93,97,101,113,117,121,125]
N = 12
F, TK = 32, 128
def setup_inputs(rng):
    return {"x": rng.standard_normal((N, 128, N * TK), dtype=np.float32).astype(ml_dtypes.bfloat16), "w": rng.standard_normal((N, 128, F), dtype=np.float32).astype(ml_dtypes.bfloat16)}
def setup_inputs_big(rng):
    d = setup_inputs(rng)
    for k in ("x", "w"): d[k] = (d[k].astype(np.float32) * 1024.0).astype(d[k].dtype)
    return d
def setup_inputs_small(rng):
    d = setup_inputs(rng)
    for k in ("x", "w"): d[k] = (d[k].astype(np.float32) * (1 / 1024.0)).astype(d[k].dtype)
    return d
def reference(x, w):
    X, W = x.astype(np.float64), w.astype(np.float64)
    y = np.zeros((N, F, N * TK))
    for r in range(N):
        for j in range(N):
            y[r][:, TK * j:TK * j + TK] = W[r].T @ X[j][:, TK * r:TK * r + TK]
    return {"y": y.astype(ml_dtypes.bfloat16 if x.dtype != np.float64 else np.float64)}

@@ -1,0 +1,184 @@
+from concourse.bass import DstId, RemoteDMATransfer
+
+TK, F = 128, 32
+BANK = 512
+NCHUNK = 6
+
+K_NEAR = 4
+K_FAR = 8
+K_HOP2 = 4
+K_DIRECT = 2
+K_NEIGH = 8
+
+SCRATCH = {
+    "xs": ("sbuf", [128, 12 * TK], "bfloat16"),
+    "land": ("sbuf", [128, 12 * TK], "bfloat16"),
+    "rb": ("sbuf", [128, 2 * TK], "bfloat16"),
+    "ws": ("sbuf", [128, F], "bfloat16"),
+    "ysb": ("sbuf", [128, 12 * TK], "bfloat16"),
+    "ps": ("psum", [128, NCHUNK * BANK], "float32"),
+}
+SEMAPHORES = (["ldx", "ldw", "rin", "sent", "st"] + ["a%d" % k for k in range(NCHUNK)]
+              + ["mm%d" % k for k in range(NCHUNK)] + ["cp%d" % k for k in range(NCHUNK)])
+
+
+def _bits(mask):
+    return [e for e in range(mask.bit_length()) if (mask >> e) & 1]
+
+
+def _deal(topo, src, wants):
+    order = sorted(range(len(wants)), key=lambda i: len(_bits(topo.mask(src, wants[i][0]))))
+    taken, out = 0, [0] * len(wants)
+    for i in order:
+        dst, k = wants[i]
+        free = [e for e in _bits(topo.mask(src, dst)) if not (taken >> e) & 1]
+        for e in free[-k:]:
+            out[i] |= 1 << e
+        assert len(_bits(out[i])) == k
+        taken |= out[i]
+    return out
+
+
+def _routes(T, topo):
+    cores = list(T.cores)
+    everyone = range(topo.CHIPS * topo.CORES_PER_CHIP)
+    chips = []
+    for c in cores:
+        if topo.chip(c) not in chips:
+            chips.append(topo.chip(c))
+    members = {t: [r for r in range(len(cores)) if topo.chip(cores[r]) == t] for t in chips}
+    taken = set(cores)
+    relay = {}
+
+    def idle(u):
+        return u not in chips
+
+    def idle_with_mate(u):
+        return idle(u) and not any(topo.mates(u, v) for v in chips)
+
+    def fits(q, j, t):
+        return (q not in taken and topo.die(q) == topo.die(cores[j]) and topo.may_write(cores[j], q)
+                and all(topo.may_write(q, cores[r]) for r in members[t]))
+
+    for j in range(len(cores)):
+        s = topo.chip(cores[j])
+        cross = [t for t in chips if t != s and not topo.may_write(cores[j], cores[members[t][0]])]
+        cross.sort(key=lambda t: not topo.mates(s, t))
+        near = [q for q in everyone if topo.chip(q) == s and all(fits(q, j, t) for t in cross)]
+        n_far = max(0, len(cross) - len(near))
+        far = {}
+        for t in cross:
+            cand = [q for q in everyone if idle(topo.chip(q)) and topo.mates(topo.chip(q), t) and fits(q, j, t)]
+            if len(far) < n_far and not topo.mates(s, t) and cand:
+                far[t] = cand[0]
+                taken.add(cand[0])
+        for t in reversed(cross):
+            cand = [q for q in everyone if idle_with_mate(topo.chip(q)) and fits(q, j, t)]
+            if len(far) < n_far and t not in far and not topo.mates(s, t):
+                far[t] = cand[0]
+                taken.add(cand[0])
+        for t, q in zip([t for t in cross if t not in far], near):
+            relay[(j, t)] = q
+            taken.add(q)
+        for t in far:
+            relay[(j, t)] = far[t]
+    return cores, chips, members, relay
+
+
+def _hop1(topo, cores, chips, relay, j):
+    ts = [t for t in chips if (j, t) in relay]
+    wants = [(relay[(j, t)], K_NEAR if topo.chip(relay[(j, t)]) == topo.chip(cores[j]) else K_FAR) for t in ts]
+    return [(t, w[0], m) for t, w, m in zip(ts, wants, _deal(topo, cores[j], wants))]
+
+
+def _k_last(topo, cores, relay, j, r):
+    if (j, topo.chip(cores[r])) in relay:
+        return K_HOP2
+    return K_NEIGH if topo.chip(cores[j]) == topo.chip(cores[r]) else K_DIRECT
+
+
+def _xfer(topo, dst_core, mask, sem, src, dst):
+    rid, pid, _ = topo.addr(dst_core)
+    return RemoteDMATransfer(dst_ids=[DstId(rid=rid, pnc=pid)], dma_engine_mask=mask, remote_sem=sem, src=src, dst=dst)
+
+
+def _blk(buf, i, n=1):
+    return buf[:, i * TK:(i + n) * TK]
+
+
+def rank_program(g, core, T, topo):
+    cores, chips, members, relay = _routes(T, topo)
+    rank = T.rank_of(core)
+
+    if rank is None:
+        mine = [jt for jt in relay if relay[jt] == core]
+        if not mine:
+            return
+        j, t = mine[0]
+        k_in = [len(_bits(m)) for tt, q, m in _hop1(topo, cores, chips, relay, j) if q == core][0]
+        wants = [(cores[r], K_HOP2) for r in members[t]]
+        masks = _deal(topo, core, wants)
+        sem = T.sem["a%d" % chips.index(topo.chip(cores[j]))]
+        g.wait_ge(T.sem.rin, k_in)
+        g.remote_dma_fused([_xfer(topo, cores[r], m, sem, _blk(T.rb, i), _blk(T.land, j))
+                            for i, (r, m) in enumerate(zip(members[t], masks))], local_sem=T.sem.sent)
+        g.wait_ge(T.sem.sent, sum(len(_bits(m)) for m in masks))
+        return
+
+    my_chip = topo.chip(core)
+    g.sync.dma_start(T.xs[:], T.x[:]).then_inc(T.sem.ldx, 16)
+    g.sync.dma_start(T.ws[:], T.w[:]).then_inc(T.sem.ldw, 16)
+
+    arr = T.sem["a%d" % chips.index(my_chip)]
+    sent = 0
+    g.wait_ge(T.sem.ldx, 16)
+    hop1 = _hop1(topo, cores, chips, relay, rank)
+    g.remote_dma_fused([_xfer(topo, q, m, T.sem.rin, _blk(T.xs, members[t][0], len(members[t])), T.rb[:])
+                        for t, q, m in hop1], local_sem=T.sem.sent)
+    sent += sum(len(_bits(m)) for t, q, m in hop1)
+    direct = [r for r in range(len(cores)) if r != rank and (rank, topo.chip(cores[r])) not in relay]
+    masks = _deal(topo, core, [(cores[r], _k_last(topo, cores, relay, rank, r)) for r in direct])
+    g.remote_dma_fused([_xfer(topo, cores[r], m, arr, _blk(T.xs, r), _blk(T.land, rank))
+                        for r, m in zip(direct, masks)], local_sem=T.sem.sent)
+    sent += sum(len(_bits(m)) for m in masks)
+
+    def lateness(s):
+        if s == my_chip:
+            return 0
+        j = members[s][0]
+        if (j, my_chip) not in relay:
+            return 1
+        if topo.chip(relay[(j, my_chip)]) != s:
+            return 4
+        return 2 if topo.mates(s, my_chip) else 3
+
+    order = sorted(chips, key=lateness)
+    g.tensor.wait_ge(T.sem.ldw, 16)
+    for n, s in enumerate(order):
+        c = chips.index(s)
+        js = members[s]
+        a, mm, cp = T.sem["a%d" % c], T.sem["mm%d" % c], T.sem["cp%d" % c]
+        width = len(js) * TK
+        due = sum(_k_last(topo, cores, relay, j, rank) for j in js if j != rank)
+        if s == my_chip:
+            g.tensor.wait_ge(T.sem.ldx, 16)
+            g.tensor.wait_ge(a, due)
+            for i, j in enumerate(js):
+                g.tensor.matmul(T.ps[0:F, c * BANK + i * TK:c * BANK + (i + 1) * TK], T.ws[:],
+                                _blk(T.xs if j == rank else T.land, j), True, True).then_inc(mm, 1)
+            n_mm = len(js)
+        else:
+            g.tensor.wait_ge(a, due)
+            g.tensor.matmul(T.ps[0:F, c * BANK:c * BANK + width], T.ws[:], _blk(T.land, js[0], len(js)),
+                            True, True).then_inc(mm, 1)
+            n_mm = 1
+        g.vector.wait_ge(mm, n_mm)
+        g.vector.tensor_copy(T.ysb[0:F, js[0] * TK:js[0] * TK + width],
+                             T.ps[0:F, c * BANK:c * BANK + width]).then_inc(cp, 1)
+        q = g.sync if n % 2 else g.scalar
+        q.wait_ge(cp, 1)
+        q.dma_start(T.y[:, js[0] * TK:js[0] * TK + width],
+                    T.ysb[0:F, js[0] * TK:js[0] * TK + width]).then_inc(T.sem.st, 16)
+
+    g.wait_ge(T.sem.sent, sent)
+    g.wait_ge(T.sem.st, 16 * len(order))

@@ -9,6 +9,7 @@ K_FAR = 8
 K_HOP2 = 4
 K_DIRECT = 2
 K_NEIGH = 8
+LATE = {"own": 0, "plane": 1, "mate": 2, "near": 3, "far": 4}
 
 SCRATCH = {
     "xs": ("sbuf", [128, 12 * TK], "bfloat16"),
@@ -18,7 +19,7 @@ SCRATCH = {
     "ysb": ("sbuf", [128, 12 * TK], "bfloat16"),
     "ps": ("psum", [128, NCHUNK * BANK], "float32"),
 }
-SEMAPHORES = (["ldx", "ldw", "rin", "sent", "st"] + ["a%d" % k for k in range(NCHUNK)]
+SEMAPHORES = (["ldf", "ldn", "lds", "ldw", "rin", "sent", "st"] + ["a%d" % k for k in range(NCHUNK)]
               + ["mm%d" % k for k in range(NCHUNK)] + ["cp%d" % k for k in range(NCHUNK)])
 
 
@@ -102,6 +103,16 @@ def _xfer(topo, dst_core, mask, sem, src, dst):
     return RemoteDMATransfer(dst_ids=[DstId(rid=rid, pnc=pid)], dma_engine_mask=mask, remote_sem=sem, src=src, dst=dst)
 
 
+def _runs(rs):
+    out = []
+    for r in rs:
+        if out and out[-1][0] + out[-1][1] == r:
+            out[-1][1] += 1
+        else:
+            out.append([r, 1])
+    return out
+
+
 def _blk(buf, i, n=1):
     return buf[:, i * TK:(i + n) * TK]
 
@@ -126,31 +137,45 @@ def rank_program(g, core, T, topo):
         return
 
     my_chip = topo.chip(core)
-    g.sync.dma_start(T.xs[:], T.x[:]).then_inc(T.sem.ldx, 16)
-    g.sync.dma_start(T.ws[:], T.w[:]).then_inc(T.sem.ldw, 16)
+    everyone = range(len(cores))
+    hop1 = _hop1(topo, cores, chips, relay, rank)
+    part = {"ldf": [h for h in hop1 if topo.chip(h[1]) != my_chip], "ldn": [h for h in hop1 if topo.chip(h[1]) == my_chip]}
+    group = {name: sorted(r for h in part[name] for r in members[h[0]]) for name in part}
+    group["lds"] = [r for r in everyone if (rank, topo.chip(cores[r])) not in relay]
+    n_load = {}
+    turn = 0
+    for name in ("ldf", "ldn", "lds"):
+        n_load[name] = 0
+        for r0, cnt in _runs(group[name]):
+            (g.scalar if turn % 2 else g.sync).dma_start(_blk(T.xs, r0, cnt),
+                                                         _blk(T.x, r0, cnt)).then_inc(T.sem[name], 16)
+            n_load[name] += 16
+            turn += 1
+    (g.scalar if turn % 2 else g.sync).dma_start(T.ws[:], T.w[:]).then_inc(T.sem.ldw, 16)
 
     arr = T.sem["a%d" % chips.index(my_chip)]
     sent = 0
-    g.wait_ge(T.sem.ldx, 16)
-    hop1 = _hop1(topo, cores, chips, relay, rank)
-    g.remote_dma_fused([_xfer(topo, q, m, T.sem.rin, _blk(T.xs, members[t][0], len(members[t])), T.rb[:])
-                        for t, q, m in hop1], local_sem=T.sem.sent)
-    sent += sum(len(_bits(m)) for t, q, m in hop1)
-    direct = [r for r in range(len(cores)) if r != rank and (rank, topo.chip(cores[r])) not in relay]
+    for name in ("ldf", "ldn"):
+        g.wait_ge(T.sem[name], n_load[name])
+        g.remote_dma_fused([_xfer(topo, q, m, T.sem.rin, _blk(T.xs, members[t][0], len(members[t])), T.rb[:])
+                            for t, q, m in part[name]], local_sem=T.sem.sent)
+        sent += sum(len(_bits(m)) for t, q, m in part[name])
+    direct = [r for r in everyone if r != rank and (rank, topo.chip(cores[r])) not in relay]
     masks = _deal(topo, core, [(cores[r], _k_last(topo, cores, relay, rank, r)) for r in direct])
+    g.wait_ge(T.sem.lds, n_load["lds"])
     g.remote_dma_fused([_xfer(topo, cores[r], m, arr, _blk(T.xs, r), _blk(T.land, rank))
                         for r, m in zip(direct, masks)], local_sem=T.sem.sent)
     sent += sum(len(_bits(m)) for m in masks)
 
     def lateness(s):
         if s == my_chip:
-            return 0
+            return LATE["own"]
         j = members[s][0]
         if (j, my_chip) not in relay:
-            return 1
+            return LATE["plane"]
         if topo.chip(relay[(j, my_chip)]) != s:
-            return 4
-        return 2 if topo.mates(s, my_chip) else 3
+            return LATE["far"]
+        return LATE["mate"] if topo.mates(s, my_chip) else LATE["near"]
 
     order = sorted(chips, key=lateness)
     g.tensor.wait_ge(T.sem.ldw, 16)
@@ -161,7 +186,7 @@ def rank_program(g, core, T, topo):
         width = len(js) * TK
         due = sum(_k_last(topo, cores, relay, j, rank) for j in js if j != rank)
         if s == my_chip:
-            g.tensor.wait_ge(T.sem.ldx, 16)
+            g.tensor.wait_ge(T.sem.lds, n_load["lds"])
             g.tensor.wait_ge(a, due)
             for i, j in enumerate(js):
                 g.tensor.matmul(T.ps[0:F, c * BANK + i * TK:c * BANK + (i + 1) * TK], T.ws[:],

from concourse.bass import DstId, RemoteDMATransfer

TK, F = 128, 32
BANK = 512
NCHUNK = 6

K_NEAR = 4
K_FAR = 8
K_HOP2 = 4
K_DIRECT = 2
K_NEIGH = 8
LATE = {"own": 0, "plane": 1, "mate": 2, "near": 3, "far": 4}

SCRATCH = {
    "xs": ("sbuf", [128, 12 * TK], "bfloat16"),
    "land": ("sbuf", [128, 12 * TK], "bfloat16"),
    "rb": ("sbuf", [128, 2 * TK], "bfloat16"),
    "ws": ("sbuf", [128, F], "bfloat16"),
    "ysb": ("sbuf", [128, 12 * TK], "bfloat16"),
    "ps": ("psum", [128, NCHUNK * BANK], "float32"),
}
SEMAPHORES = (["ldf", "ldn", "lds", "ldw", "rin", "sent", "st"] + ["a%d" % k for k in range(NCHUNK)]
              + ["mm%d" % k for k in range(NCHUNK)] + ["cp%d" % k for k in range(NCHUNK)])


def _bits(mask):
    return [e for e in range(mask.bit_length()) if (mask >> e) & 1]


def _deal(topo, src, wants):
    order = sorted(range(len(wants)), key=lambda i: len(_bits(topo.mask(src, wants[i][0]))))
    taken, out = 0, [0] * len(wants)
    for i in order:
        dst, k = wants[i]
        free = [e for e in _bits(topo.mask(src, dst)) if not (taken >> e) & 1]
        for e in free[-k:]:
            out[i] |= 1 << e
        assert len(_bits(out[i])) == k
        taken |= out[i]
    return out


def _routes(T, topo):
    cores = list(T.cores)
    everyone = range(topo.CHIPS * topo.CORES_PER_CHIP)
    chips = []
    for c in cores:
        if topo.chip(c) not in chips:
            chips.append(topo.chip(c))
    members = {t: [r for r in range(len(cores)) if topo.chip(cores[r]) == t] for t in chips}
    taken = set(cores)
    relay = {}

    def idle(u):
        return u not in chips

    def idle_with_mate(u):
        return idle(u) and not any(topo.mates(u, v) for v in chips)

    def fits(q, j, t):
        return (q not in taken and topo.die(q) == topo.die(cores[j]) and topo.may_write(cores[j], q)
                and all(topo.may_write(q, cores[r]) for r in members[t]))

    for j in range(len(cores)):
        s = topo.chip(cores[j])
        cross = [t for t in chips if t != s and not topo.may_write(cores[j], cores[members[t][0]])]
        cross.sort(key=lambda t: not topo.mates(s, t))
        near = [q for q in everyone if topo.chip(q) == s and all(fits(q, j, t) for t in cross)]
        n_far = max(0, len(cross) - len(near))
        far = {}
        for t in cross:
            cand = [q for q in everyone if idle(topo.chip(q)) and topo.mates(topo.chip(q), t) and fits(q, j, t)]
            if len(far) < n_far and not topo.mates(s, t) and cand:
                far[t] = cand[0]
                taken.add(cand[0])
        for t in reversed(cross):
            cand = [q for q in everyone if idle_with_mate(topo.chip(q)) and fits(q, j, t)]
            if len(far) < n_far and t not in far and not topo.mates(s, t):
                far[t] = cand[0]
                taken.add(cand[0])
        for t, q in zip([t for t in cross if t not in far], near):
            relay[(j, t)] = q
            taken.add(q)
        for t in far:
            relay[(j, t)] = far[t]
    return cores, chips, members, relay


def _hop1(topo, cores, chips, relay, j):
    ts = [t for t in chips if (j, t) in relay]
    wants = [(relay[(j, t)], K_NEAR if topo.chip(relay[(j, t)]) == topo.chip(cores[j]) else K_FAR) for t in ts]
    return [(t, w[0], m) for t, w, m in zip(ts, wants, _deal(topo, cores[j], wants))]


def _k_last(topo, cores, relay, j, r):
    if (j, topo.chip(cores[r])) in relay:
        return K_HOP2
    return K_NEIGH if topo.chip(cores[j]) == topo.chip(cores[r]) else K_DIRECT


def _xfer(topo, dst_core, mask, sem, src, dst):
    rid, pid, _ = topo.addr(dst_core)
    return RemoteDMATransfer(dst_ids=[DstId(rid=rid, pnc=pid)], dma_engine_mask=mask, remote_sem=sem, src=src, dst=dst)


def _runs(rs):
    out = []
    for r in rs:
        if out and out[-1][0] + out[-1][1] == r:
            out[-1][1] += 1
        else:
            out.append([r, 1])
    return out


def _blk(buf, i, n=1):
    return buf[:, i * TK:(i + n) * TK]


def rank_program(g, core, T, topo):
    cores, chips, members, relay = _routes(T, topo)
    rank = T.rank_of(core)

    if rank is None:
        mine = [jt for jt in relay if relay[jt] == core]
        if not mine:
            return
        j, t = mine[0]
        k_in = [len(_bits(m)) for tt, q, m in _hop1(topo, cores, chips, relay, j) if q == core][0]
        wants = [(cores[r], K_HOP2) for r in members[t]]
        masks = _deal(topo, core, wants)
        sem = T.sem["a%d" % chips.index(topo.chip(cores[j]))]
        g.wait_ge(T.sem.rin, k_in)
        g.remote_dma_fused([_xfer(topo, cores[r], m, sem, _blk(T.rb, i), _blk(T.land, j))
                            for i, (r, m) in enumerate(zip(members[t], masks))], local_sem=T.sem.sent)
        g.wait_ge(T.sem.sent, sum(len(_bits(m)) for m in masks))
        return

    my_chip = topo.chip(core)
    everyone = range(len(cores))
    hop1 = _hop1(topo, cores, chips, relay, rank)
    part = {"ldf": [h for h in hop1 if topo.chip(h[1]) != my_chip], "ldn": [h for h in hop1 if topo.chip(h[1]) == my_chip]}
    group = {name: sorted(r for h in part[name] for r in members[h[0]]) for name in part}
    group["lds"] = [r for r in everyone if (rank, topo.chip(cores[r])) not in relay]
    n_load = {}
    turn = 0
    for name in ("ldf", "ldn", "lds"):
        n_load[name] = 0
        for r0, cnt in _runs(group[name]):
            (g.scalar if turn % 2 else g.sync).dma_start(_blk(T.xs, r0, cnt),
                                                         _blk(T.x, r0, cnt)).then_inc(T.sem[name], 16)
            n_load[name] += 16
            turn += 1
    (g.scalar if turn % 2 else g.sync).dma_start(T.ws[:], T.w[:]).then_inc(T.sem.ldw, 16)

    arr = T.sem["a%d" % chips.index(my_chip)]
    sent = 0
    for name in ("ldf", "ldn"):
        g.wait_ge(T.sem[name], n_load[name])
        g.remote_dma_fused([_xfer(topo, q, m, T.sem.rin, _blk(T.xs, members[t][0], len(members[t])), T.rb[:])
                            for t, q, m in part[name]], local_sem=T.sem.sent)
        sent += sum(len(_bits(m)) for t, q, m in part[name])
    direct = [r for r in everyone if r != rank and (rank, topo.chip(cores[r])) not in relay]
    masks = _deal(topo, core, [(cores[r], _k_last(topo, cores, relay, rank, r)) for r in direct])
    g.wait_ge(T.sem.lds, n_load["lds"])
    g.remote_dma_fused([_xfer(topo, cores[r], m, arr, _blk(T.xs, r), _blk(T.land, rank))
                        for r, m in zip(direct, masks)], local_sem=T.sem.sent)
    sent += sum(len(_bits(m)) for m in masks)

    def lateness(s):
        if s == my_chip:
            return LATE["own"]
        j = members[s][0]
        if (j, my_chip) not in relay:
            return LATE["plane"]
        if topo.chip(relay[(j, my_chip)]) != s:
            return LATE["far"]
        return LATE["mate"] if topo.mates(s, my_chip) else LATE["near"]

    order = sorted(chips, key=lateness)
    g.tensor.wait_ge(T.sem.ldw, 16)
    for n, s in enumerate(order):
        c = chips.index(s)
        js = members[s]
        a, mm, cp = T.sem["a%d" % c], T.sem["mm%d" % c], T.sem["cp%d" % c]
        width = len(js) * TK
        due = sum(_k_last(topo, cores, relay, j, rank) for j in js if j != rank)
        if s == my_chip:
            g.tensor.wait_ge(T.sem.lds, n_load["lds"])
            g.tensor.wait_ge(a, due)
            for i, j in enumerate(js):
                g.tensor.matmul(T.ps[0:F, c * BANK + i * TK:c * BANK + (i + 1) * TK], T.ws[:],
                                _blk(T.xs if j == rank else T.land, j), True, True).then_inc(mm, 1)
            n_mm = len(js)
        else:
            g.tensor.wait_ge(a, due)
            g.tensor.matmul(T.ps[0:F, c * BANK:c * BANK + width], T.ws[:], _blk(T.land, js[0], len(js)),
                            True, True).then_inc(mm, 1)
            n_mm = 1
        g.vector.wait_ge(mm, n_mm)
        g.vector.tensor_copy(T.ysb[0:F, js[0] * TK:js[0] * TK + width],
                             T.ps[0:F, c * BANK:c * BANK + width]).then_inc(cp, 1)
        q = g.sync if n % 2 else g.scalar
        q.wait_ge(cp, 1)
        q.dma_start(T.y[:, js[0] * TK:js[0] * TK + width],
                    T.ysb[0:F, js[0] * TK:js[0] * TK + width]).then_inc(T.sem.st, 16)

    g.wait_ge(T.sem.sent, sent)
    g.wait_ge(T.sem.st, 16 * len(order))
